import numpy as np, ml_dtypes
CORES = [52,68,84,180,196,212,308,324,340]
N = 9
TOK, K = 256, 2
EPS = 0.01
ROUTE = [[[4,8],[2,8],[2,6],[1,3],[1,7],[0,8],[4,8],[1,7],[1,6],[1,7],[1,5],[0,3],[1,5],[1,8],[0,1],[1,4],[6,7],[0,2],[3,5],[5,6],[3,5],[1,2],[3,7],[5,8],[0,1],[0,6],[1,5],[0,1],[0,6],[0,8],[2,6],[1,5],[7,8],[0,8],[1,6],[0,1],[4,6],[2,5],[3,8],[3,7],[0,2],[0,7],[1,6],[0,8],[1,4],[1,5],[2,3],[3,7],[4,5],[5,8],[5,6],[0,3],[6,8],[0,2],[5,7],[0,1],[1,6],[0,4],[0,1],[3,5],[3,6],[0,1],[2,3],[1,2],[2,8],[3,6],[1,7],[0,2],[1,3],[0,1],[1,5],[4,6],[1,5],[5,8],[4,5],[1,6],[0,5],[0,2],[5,8],[0,4],[5,8],[5,8],[0,5],[7,8],[4,8],[5,7],[4,6],[2,8],[0,8],[7,8],[5,7],[3,8],[1,6],[2,4],[4,5],[7,8],[1,5],[6,8],[4,6],[6,7],[1,5],[5,8],[1,7],[3,7],[1,5],[4,6],[0,1],[1,6],[1,6],[0,5],[5,7],[3,7],[0,8],[2,8],[6,8],[0,6],[6,7],[2,4],[0,5],[6,7],[0,4],[5,6],[1,2],[0,5],[0,2],[1,6],[0,3],[7,8],[0,5],[4,7],[5,8],[1,3],[5,7],[5,6],[3,4],[5,6],[2,5],[5,6],[6,8],[0,5],[5,8],[2,8],[1,6],[0,5],[4,5],[7,8],[5,7],[6,8],[0,5],[3,8],[3,7],[3,7],[2,6],[0,3],[3,7],[1,8],[1,3],[1,3],[2,6],[4,6],[2,4],[0,1],[3,4],[6,8],[3,7],[2,5],[3,6],[0,2],[4,5],[3,6],[3,8],[7,8],[3,6],[4,5],[0,7],[3,4],[3,5],[2,4],[3,6],[1,8],[3,8],[1,6],[1,5],[4,8],[3,4],[2,3],[5,6],[3,6],[2,3],[1,5],[0,3],[5,7],[2,4],[1,2],[2,7],[1,7],[4,7],[2,5],[6,7],[1,7],[1,8],[3,7],[4,8],[0,6],[2,8],[2,5],[2,6],[0,6],[0,7],[1,3],[7,8],[0,3],[5,6],[1,7],[1,8],[0,8],[1,3],[3,7],[1,7],[0,1],[3,6],[1,8],[5,7],[1,5],[1,7],[1,8],[3,5],[3,7],[0,6],[6,8],[6,8],[3,4],[1,5],[0,3],[4,7],[1,5],[0,6],[3,5],[4,7],[4,8],[3,6],[0,1],[2,3],[0,5],[2,3],[7,8],[2,5],[0,8],[1,8],[0,2],[2,5],[3,8],[4,6],[1,2],[1,8],[0,5]],[[0,4],[0,7],[4,6],[3,6],[2,4],[2,4],[0,8],[5,8],[3,7],[2,7],[1,4],[1,2],[4,5],[1,7],[3,6],[3,5],[7,8],[1,2],[4,7],[3,4],[1,5],[5,6],[4,6],[5,7],[5,7],[0,1],[2,8],[0,2],[0,1],[5,8],[2,7],[5,7],[1,4],[5,8],[6,8],[4,7],[3,5],[5,6],[3,6],[1,8],[3,5],[7,8],[7,8],[1,6],[0,7],[2,8],[0,7],[2,6],[0,4],[2,8],[5,7],[0,5],[3,8],[1,5],[0,1],[4,5],[3,4],[1,3],[7,8],[4,6],[1,8],[5,8],[4,8],[2,7],[4,5],[1,3],[7,8],[4,8],[6,7],[2,7],[0,7],[6,7],[2,3],[4,5],[1,2],[7,8],[0,6],[3,8],[5,7],[4,7],[6,7],[6,7],[4,8],[5,7],[2,4],[0,4],[1,8],[7,8],[5,7],[2,5],[4,5],[4,8],[7,8],[0,1],[3,5],[0,2],[2,4],[0,7],[1,5],[6,8],[1,4],[2,7],[0,4],[3,8],[0,1],[7,8],[3,8],[5,6],[2,4],[1,5],[1,4],[0,4],[0,4],[3,4],[0,5],[4,8],[2,6],[0,1],[4,5],[3,6],[0,7],[1,8],[1,6],[3,7],[2,6],[1,6],[0,3],[4,8],[4,7],[0,8],[3,4],[0,1],[5,6],[3,7],[4,6],[0,1],[1,3],[0,7],[4,7],[1,4],[0,4],[1,8],[2,5],[7,8],[1,5],[0,8],[0,8],[2,8],[3,7],[2,7],[3,5],[3,7],[0,3],[5,8],[0,7],[1,8],[1,2],[0,5],[4,7],[2,7],[4,8],[5,7],[0,2],[1,2],[6,7],[1,5],[5,6],[3,7],[1,5],[0,6],[1,3],[1,4],[0,7],[6,7],[3,7],[2,4],[2,5],[7,8],[0,7],[1,2],[3,7],[5,6],[3,8],[0,2],[0,2],[2,4],[3,5],[2,6],[6,7],[6,8],[5,6],[4,5],[1,8],[1,5],[0,6],[0,7],[0,5],[0,1],[6,7],[0,6],[0,6],[7,8],[0,3],[0,5],[1,7],[3,5],[6,7],[6,8],[2,8],[3,4],[1,7],[0,4],[5,6],[4,5],[0,7],[6,8],[0,5],[5,7],[3,7],[2,4],[5,6],[5,7],[1,3],[2,5],[3,5],[4,6],[0,4],[3,5],[1,8],[3,4],[4,8],[2,8],[4,7],[6,8],[5,6],[4,5],[3,6],[4,5],[7,8],[0,5],[0,5],[4,8],[3,4],[5,6],[3,6],[2,3],[2,7],[4,6],[1,2],[4,8],[0,2],[0,4],[5,7],[1,4],[4,7],[4,7]],[[1,3],[0,4],[4,7],[5,6],[0,8],[4,5],[1,2],[0,6],[5,8],[6,8],[1,7],[5,7],[3,6],[1,8],[0,2],[5,8],[0,5],[2,6],[0,4],[2,3],[0,7],[4,6],[2,4],[2,3],[1,5],[1,3],[6,8],[3,5],[0,8],[0,4],[6,8],[0,3],[6,7],[1,5],[2,7],[1,8],[3,7],[6,8],[5,8],[0,2],[1,5],[6,7],[4,5],[1,3],[0,7],[0,6],[2,6],[5,6],[2,7],[3,4],[0,6],[0,5],[0,8],[7,8],[2,3],[1,4],[1,5],[0,2],[3,6],[3,4],[3,4],[2,7],[0,3],[6,8],[2,6],[6,8],[1,7],[7,8],[6,7],[1,3],[6,7],[2,8],[5,8],[2,4],[3,6],[3,5],[2,8],[3,5],[1,3],[4,7],[0,7],[2,6],[4,5],[3,7],[0,2],[3,7],[0,1],[0,7],[7,8],[1,5],[2,5],[1,4],[1,4],[4,5],[3,8],[2,7],[5,7],[2,8],[1,7],[0,4],[2,8],[2,8],[1,3],[5,6],[1,6],[7,8],[1,3],[1,3],[2,7],[5,7],[5,8],[3,6],[1,8],[2,4],[6,7],[3,8],[1,4],[5,6],[1,2],[3,5],[4,6],[0,4],[7,8],[2,7],[2,5],[1,2],[0,8],[0,8],[2,5],[5,7],[6,8],[2,6],[6,7],[4,8],[3,4],[2,3],[4,5],[1,3],[1,6],[5,8],[6,8],[2,3],[2,8],[2,7],[1,8],[2,7],[1,5],[1,6],[2,3],[2,8],[4,7],[6,7],[3,5],[2,8],[3,4],[4,6],[3,6],[2,3],[0,8],[0,7],[2,4],[0,1],[1,6],[4,6],[2,5],[1,5],[4,6],[2,8],[2,8],[4,7],[0,5],[4,5],[2,7],[5,7],[5,6],[0,1],[3,8],[3,7],[6,8],[3,7],[1,5],[3,6],[1,3],[4,7],[4,5],[3,7],[1,5],[0,1],[3,6],[0,4],[1,3],[1,8],[0,2],[1,8],[5,6],[0,3],[1,3],[0,5],[3,6],[7,8],[5,8],[5,6],[5,8],[6,7],[1,7],[2,3],[5,7],[1,7],[3,7],[2,3],[0,5],[2,4],[1,4],[2,4],[2,8],[3,7],[2,4],[5,6],[0,1],[1,6],[1,2],[5,7],[1,8],[1,6],[1,8],[0,2],[2,7],[5,8],[3,6],[7,8],[4,8],[3,7],[2,5],[4,8],[4,6],[0,6],[1,3],[3,7],[0,6],[4,7],[4,8],[4,5],[0,4],[5,8],[3,5],[1,4],[0,7],[0,8],[6,7],[3,5],[3,7],[5,7],[3,5],[0,3],[0,4],[0,3]],[[4,6],[7,8],[0,2],[4,5],[4,5],[5,7],[3,6],[1,4],[0,8],[3,4],[1,2],[5,8],[2,7],[2,4],[1,8],[2,5],[1,5],[6,7],[0,3],[6,7],[1,3],[5,7],[1,3],[2,6],[2,6],[2,6],[2,3],[4,8],[0,3],[1,6],[4,8],[0,5],[2,6],[7,8],[1,3],[0,3],[0,8],[7,8],[0,6],[2,8],[0,8],[6,7],[3,8],[1,7],[0,5],[1,4],[0,3],[5,7],[0,7],[0,3],[6,7],[5,6],[0,4],[1,7],[1,8],[1,4],[2,6],[3,4],[2,7],[4,7],[0,1],[1,3],[3,4],[6,7],[1,2],[1,3],[0,5],[0,5],[5,8],[2,7],[4,5],[0,7],[6,8],[0,6],[1,8],[4,7],[2,4],[0,4],[0,7],[1,7],[0,5],[2,5],[0,6],[1,4],[1,2],[2,7],[5,8],[0,5],[2,3],[4,5],[4,7],[6,7],[5,8],[3,4],[7,8],[6,7],[0,3],[2,7],[1,2],[3,4],[3,4],[0,3],[1,2],[3,7],[3,4],[2,5],[4,7],[1,3],[1,8],[0,7],[1,4],[3,5],[5,6],[0,5],[1,8],[2,6],[0,6],[5,6],[1,6],[0,7],[3,6],[0,3],[4,7],[2,4],[0,1],[3,8],[2,5],[0,4],[2,4],[2,6],[3,7],[1,6],[3,7],[6,8],[4,7],[4,8],[1,6],[2,6],[4,5],[2,5],[0,1],[7,8],[2,7],[1,7],[5,7],[2,6],[0,6],[2,3],[5,7],[1,8],[1,6],[2,7],[2,4],[3,8],[3,4],[1,5],[0,2],[0,6],[5,7],[0,7],[2,6],[3,6],[7,8],[7,8],[4,7],[0,6],[2,5],[0,7],[0,7],[1,5],[1,6],[4,8],[3,7],[0,7],[0,2],[2,7],[1,4],[1,5],[5,7],[2,4],[0,5],[1,8],[1,5],[0,4],[0,8],[2,6],[1,4],[3,5],[3,6],[0,2],[2,7],[2,7],[3,4],[1,5],[1,4],[0,1],[4,6],[3,4],[0,5],[2,4],[0,1],[3,5],[6,7],[0,5],[1,3],[2,7],[5,7],[1,2],[4,7],[0,5],[3,4],[0,1],[2,3],[1,8],[1,6],[3,6],[1,7],[2,3],[0,3],[2,5],[6,8],[4,5],[5,7],[7,8],[2,7],[1,5],[3,8],[1,4],[4,6],[3,7],[3,7],[0,3],[0,3],[2,4],[0,6],[6,8],[5,6],[3,6],[0,5],[7,8],[1,7],[0,2],[3,8],[4,8],[2,8],[1,8],[1,3],[0,1],[4,8],[1,2],[0,8],[0,2],[2,5],[1,3],[5,8],[0,2]],[[6,7],[1,2],[4,8],[0,1],[1,6],[3,6],[0,2],[0,6],[1,8],[2,3],[4,7],[7,8],[3,5],[2,3],[1,8],[3,5],[4,6],[2,7],[1,3],[2,4],[1,2],[4,5],[0,3],[4,6],[1,6],[1,8],[1,6],[0,8],[6,8],[0,6],[4,8],[0,8],[3,5],[2,6],[5,8],[5,8],[2,5],[0,6],[4,7],[6,8],[0,4],[1,6],[2,7],[0,3],[0,5],[4,6],[0,7],[4,7],[3,4],[1,8],[4,7],[4,6],[0,2],[0,2],[0,6],[3,7],[0,4],[6,7],[2,3],[3,6],[0,4],[0,4],[1,3],[1,4],[4,8],[1,5],[0,7],[2,7],[3,4],[1,3],[1,2],[7,8],[0,6],[4,5],[0,4],[1,6],[6,7],[3,4],[1,2],[1,5],[7,8],[0,6],[3,4],[2,5],[0,7],[0,7],[5,7],[0,2],[4,6],[3,4],[0,4],[6,7],[1,2],[1,6],[2,4],[3,5],[5,8],[5,8],[0,6],[0,3],[6,7],[1,7],[3,4],[1,4],[7,8],[0,4],[3,8],[4,5],[0,5],[0,8],[0,5],[2,6],[3,8],[6,7],[5,7],[5,6],[3,8],[0,7],[2,5],[6,8],[1,6],[4,7],[3,7],[1,8],[4,8],[3,7],[1,5],[4,7],[1,8],[5,8],[2,4],[4,7],[6,8],[4,8],[0,1],[0,4],[1,5],[1,2],[7,8],[6,8],[7,8],[3,8],[0,6],[6,7],[2,8],[4,7],[2,7],[2,7],[3,8],[1,5],[1,8],[3,6],[5,8],[3,7],[5,8],[0,3],[0,8],[3,8],[1,6],[0,7],[0,8],[4,6],[2,8],[1,5],[2,8],[0,4],[2,6],[0,1],[3,5],[5,6],[7,8],[6,8],[3,8],[6,7],[2,4],[0,8],[2,8],[0,5],[3,4],[3,8],[4,8],[2,6],[2,6],[6,8],[2,7],[1,3],[3,7],[5,8],[3,5],[5,6],[4,5],[0,8],[7,8],[5,8],[4,7],[0,5],[1,7],[1,7],[0,6],[3,7],[5,6],[0,4],[2,5],[4,8],[2,4],[3,4],[7,8],[3,8],[4,8],[3,8],[2,7],[2,5],[3,4],[6,8],[2,3],[0,1],[5,6],[4,6],[0,3],[1,2],[1,6],[4,6],[0,3],[0,3],[0,3],[4,8],[1,6],[4,6],[3,4],[4,6],[1,7],[4,5],[7,8],[3,4],[0,6],[6,7],[1,3],[6,8],[0,3],[2,3],[1,3],[6,8],[2,6],[0,6],[4,5],[0,6],[6,8],[0,7],[3,5],[5,7],[3,4],[1,3],[0,3],[0,3],[4,5],[2,8]],[[0,3],[2,8],[2,4],[1,7],[4,7],[1,7],[3,8],[2,8],[6,7],[0,8],[3,6],[2,5],[1,6],[2,3],[3,7],[6,8],[1,4],[6,7],[7,8],[0,3],[2,4],[5,6],[5,8],[0,1],[4,8],[3,4],[0,8],[3,8],[1,2],[4,6],[3,6],[1,7],[1,7],[1,4],[4,6],[3,6],[1,7],[3,8],[1,4],[0,4],[0,3],[1,7],[1,2],[1,7],[0,5],[4,5],[4,7],[1,3],[4,7],[6,7],[1,3],[3,5],[2,3],[2,8],[6,7],[1,4],[7,8],[6,8],[2,7],[0,2],[1,4],[6,8],[0,5],[1,4],[2,4],[1,8],[1,6],[4,8],[5,6],[1,5],[3,7],[6,7],[0,5],[4,7],[0,4],[3,8],[1,8],[4,5],[0,5],[2,6],[0,2],[4,6],[2,4],[3,4],[0,6],[0,1],[7,8],[3,4],[3,4],[3,5],[1,6],[7,8],[1,5],[2,5],[1,2],[4,8],[1,6],[2,3],[0,8],[3,6],[3,6],[0,6],[7,8],[0,6],[3,8],[6,7],[6,8],[4,5],[1,8],[0,4],[2,6],[2,8],[0,2],[4,5],[0,4],[7,8],[4,8],[0,1],[6,7],[2,6],[3,7],[4,8],[2,3],[0,1],[3,8],[0,7],[3,5],[2,5],[1,4],[3,4],[3,4],[7,8],[1,7],[3,4],[3,4],[6,8],[0,1],[0,6],[3,8],[5,8],[5,7],[1,3],[0,1],[3,7],[1,5],[6,7],[7,8],[0,7],[0,7],[0,2],[0,1],[3,8],[2,5],[0,1],[0,5],[5,6],[3,7],[0,3],[1,6],[5,6],[5,8],[6,8],[4,8],[5,7],[1,8],[0,3],[2,6],[1,6],[0,3],[5,6],[1,2],[1,5],[2,5],[2,4],[0,2],[2,4],[3,8],[6,7],[3,6],[2,6],[2,8],[1,7],[1,6],[2,4],[0,8],[6,7],[6,7],[0,5],[2,8],[1,7],[3,5],[7,8],[2,3],[2,8],[1,7],[4,6],[2,4],[3,6],[1,2],[1,2],[2,5],[2,7],[3,5],[2,8],[1,3],[2,6],[2,6],[0,4],[0,1],[0,5],[7,8],[3,5],[0,4],[3,7],[3,8],[2,8],[2,8],[0,7],[3,7],[2,4],[1,7],[0,1],[0,3],[2,4],[0,3],[6,8],[1,5],[3,8],[1,4],[4,5],[3,5],[2,7],[0,5],[3,5],[3,6],[1,4],[2,5],[2,6],[1,4],[0,3],[2,8],[2,5],[0,6],[3,7],[3,8],[1,2],[3,5],[3,6],[0,2],[1,2],[6,7],[6,8],[5,7],[0,1],[2,4],[0,7]],[[1,3],[2,3],[3,6],[1,7],[2,7],[1,8],[1,5],[0,7],[1,2],[5,7],[5,7],[1,3],[3,7],[1,8],[1,8],[5,8],[2,5],[4,6],[7,8],[0,1],[3,8],[6,7],[4,5],[6,7],[0,3],[3,4],[1,7],[4,8],[4,5],[4,7],[2,3],[1,2],[1,2],[4,7],[5,6],[3,8],[1,6],[4,5],[0,1],[0,8],[3,8],[6,8],[0,8],[4,5],[4,5],[7,8],[0,5],[5,7],[5,6],[2,8],[6,7],[2,7],[5,6],[2,5],[3,4],[4,8],[0,7],[0,6],[2,7],[3,6],[0,5],[4,5],[0,6],[0,8],[1,2],[0,2],[1,3],[3,4],[1,7],[0,3],[0,2],[2,7],[0,5],[2,3],[0,3],[0,1],[0,4],[0,3],[0,7],[4,6],[0,2],[0,4],[1,8],[3,4],[1,8],[0,4],[0,3],[2,4],[1,6],[5,8],[5,7],[6,8],[4,5],[3,5],[7,8],[3,8],[0,3],[3,4],[4,8],[4,6],[6,7],[1,8],[3,7],[3,5],[2,6],[3,4],[1,7],[0,1],[0,7],[2,4],[2,5],[1,5],[0,2],[1,5],[1,5],[2,7],[2,7],[1,6],[4,5],[2,3],[1,4],[0,2],[5,8],[0,5],[6,7],[5,8],[0,4],[5,8],[1,4],[2,7],[5,7],[0,7],[0,3],[1,3],[2,6],[0,3],[2,8],[0,4],[0,1],[1,3],[3,6],[0,8],[4,7],[3,4],[5,8],[2,5],[1,8],[2,4],[2,6],[4,7],[2,4],[1,5],[2,7],[4,6],[4,6],[5,7],[3,7],[4,8],[2,6],[4,5],[5,7],[0,3],[2,5],[7,8],[5,7],[6,7],[4,8],[2,7],[3,7],[2,7],[6,8],[5,8],[1,4],[3,6],[0,1],[0,2],[4,7],[7,8],[4,5],[4,8],[1,4],[1,4],[2,5],[0,7],[0,7],[2,3],[2,5],[4,8],[2,5],[3,6],[4,5],[6,8],[0,4],[1,3],[3,7],[3,5],[1,6],[1,5],[0,3],[4,8],[6,7],[2,4],[4,6],[4,6],[1,4],[1,6],[5,7],[0,6],[0,5],[0,8],[0,8],[4,8],[1,2],[3,8],[2,4],[2,4],[3,5],[2,5],[2,3],[0,1],[0,4],[7,8],[1,4],[1,6],[3,4],[4,8],[5,6],[1,4],[4,8],[4,8],[4,7],[5,7],[2,4],[0,2],[0,8],[1,5],[1,2],[2,3],[6,7],[2,7],[4,8],[3,8],[0,5],[1,4],[1,5],[2,3],[3,5],[2,7],[0,7],[0,8],[0,7],[2,8],[5,7],[6,8],[4,7],[6,8]],[[2,8],[2,7],[2,5],[5,7],[3,6],[0,3],[5,6],[1,2],[2,6],[4,5],[3,8],[2,5],[2,3],[3,8],[4,7],[0,8],[4,5],[1,2],[2,5],[4,5],[0,6],[2,8],[1,3],[0,3],[0,1],[2,8],[4,5],[5,8],[5,8],[0,4],[4,8],[0,8],[3,4],[2,5],[0,8],[3,7],[2,8],[7,8],[0,7],[2,8],[4,8],[2,5],[0,8],[0,3],[3,4],[0,6],[5,7],[0,5],[2,3],[1,4],[4,7],[6,7],[6,8],[0,7],[6,7],[4,7],[2,5],[1,3],[3,7],[1,8],[0,2],[3,7],[0,7],[1,8],[4,5],[3,4],[3,6],[3,6],[4,8],[4,7],[0,3],[0,8],[6,8],[0,6],[7,8],[1,8],[3,4],[3,4],[5,8],[1,2],[1,2],[4,7],[3,8],[1,8],[2,4],[4,5],[1,6],[3,5],[6,8],[1,8],[0,8],[1,8],[0,6],[0,2],[0,1],[0,3],[5,6],[6,7],[2,4],[4,6],[0,8],[1,5],[0,4],[0,8],[0,3],[5,7],[4,7],[0,2],[3,4],[4,8],[0,4],[4,5],[0,6],[6,8],[1,5],[2,5],[0,4],[5,8],[5,8],[2,4],[3,5],[5,7],[3,6],[7,8],[2,5],[2,4],[6,8],[0,2],[2,8],[1,7],[1,5],[2,3],[5,7],[0,1],[1,3],[2,5],[0,5],[4,8],[0,1],[3,6],[5,6],[6,7],[5,7],[2,6],[1,4],[1,4],[2,5],[2,3],[2,7],[7,8],[0,3],[3,8],[0,6],[4,8],[2,8],[0,1],[0,8],[3,4],[1,2],[1,6],[1,6],[3,6],[1,4],[3,7],[2,8],[1,4],[6,7],[4,7],[6,8],[1,7],[3,7],[1,4],[3,5],[3,5],[2,4],[1,2],[3,4],[5,7],[1,6],[6,7],[2,3],[1,8],[0,6],[1,6],[0,6],[1,3],[3,5],[3,7],[2,4],[0,4],[0,6],[2,4],[1,8],[6,7],[0,1],[0,1],[4,8],[1,5],[3,4],[3,5],[0,4],[6,8],[0,6],[1,2],[0,3],[1,3],[5,7],[0,8],[4,6],[6,8],[2,4],[3,7],[1,8],[0,5],[2,7],[1,7],[2,6],[2,6],[3,8],[5,8],[2,6],[5,6],[0,6],[2,7],[2,5],[4,7],[3,8],[5,6],[0,1],[0,1],[2,4],[3,7],[0,2],[3,4],[4,7],[0,2],[1,4],[1,6],[3,8],[1,6],[0,6],[1,4],[3,7],[1,6],[2,3],[3,5],[7,8],[3,8],[0,4],[3,6],[2,4],[2,7],[3,7],[4,6],[2,5],[3,6]],[[4,8],[2,7],[2,4],[3,7],[4,6],[2,5],[1,7],[2,7],[5,7],[1,7],[5,7],[1,6],[4,7],[0,2],[4,8],[3,6],[3,7],[1,2],[0,1],[0,1],[1,6],[1,7],[3,5],[3,6],[5,7],[1,4],[3,5],[0,8],[4,6],[7,8],[0,6],[3,5],[0,5],[1,4],[0,5],[5,6],[0,7],[0,8],[1,2],[4,6],[4,7],[5,7],[1,6],[0,7],[3,5],[5,6],[2,6],[3,8],[4,5],[2,5],[6,8],[1,8],[2,5],[2,3],[1,8],[3,4],[1,3],[5,8],[6,7],[0,1],[3,4],[1,4],[0,3],[1,3],[1,5],[7,8],[4,5],[2,3],[2,5],[3,4],[3,4],[2,3],[0,6],[0,4],[1,3],[3,5],[3,6],[1,8],[2,6],[5,8],[1,5],[4,5],[2,7],[0,6],[1,4],[0,3],[6,8],[0,6],[0,2],[3,5],[2,6],[0,7],[0,4],[6,7],[3,8],[1,3],[3,6],[5,7],[0,8],[0,7],[2,6],[4,7],[0,1],[0,6],[1,4],[4,5],[1,6],[4,8],[0,8],[6,7],[3,6],[2,3],[1,7],[0,6],[1,7],[1,3],[3,5],[0,6],[4,8],[1,2],[0,5],[0,1],[7,8],[0,6],[1,8],[1,8],[1,6],[0,2],[0,4],[0,7],[3,7],[0,3],[2,6],[3,4],[0,2],[6,7],[3,6],[3,6],[2,6],[2,6],[0,7],[1,2],[0,1],[6,8],[2,8],[0,1],[2,7],[3,7],[0,5],[3,8],[6,8],[3,8],[4,7],[0,2],[1,7],[6,8],[0,1],[1,7],[1,5],[3,4],[5,8],[6,8],[1,6],[2,3],[0,6],[7,8],[0,6],[4,6],[0,5],[2,3],[6,7],[1,2],[0,3],[1,5],[6,8],[4,7],[3,8],[3,8],[2,6],[2,8],[5,8],[1,8],[3,8],[1,3],[0,6],[4,7],[2,8],[3,7],[2,7],[0,3],[2,8],[5,7],[2,4],[2,3],[4,7],[1,4],[3,7],[3,6],[1,7],[0,2],[6,8],[3,4],[5,7],[0,3],[1,6],[1,8],[0,5],[2,4],[1,2],[3,8],[2,6],[2,6],[0,5],[4,7],[0,3],[1,5],[1,8],[5,7],[0,3],[0,6],[0,7],[1,2],[6,8],[0,5],[5,7],[6,7],[0,3],[5,6],[3,8],[0,7],[0,7],[4,7],[1,5],[1,8],[5,7],[1,8],[0,7],[2,3],[0,6],[2,6],[1,3],[0,2],[1,3],[0,4],[6,8],[4,7],[5,8],[0,2],[5,7],[0,3],[1,2],[4,5],[1,5],[5,6],[4,8],[1,3]]]
def sigmoid(z):
    a = np.exp(-np.abs(z)); return np.where(z >= 0, 1.0, a) / (1.0 + a)
def setup_inputs(rng):
    rt = (0.75 * rng.standard_normal((128, 1), dtype=np.float32) + rng.standard_normal((128, N), dtype=np.float32) / 2).astype(ml_dtypes.bfloat16)
    rm = np.zeros((N, N, TOK), np.float32)
    for r in range(N):
        for t in range(TOK): rm[r, ROUTE[r][t], t] = 1.0
    return {"x": (rng.standard_normal((N, 128, TOK), dtype=np.float32) / 8).astype(ml_dtypes.bfloat16), "rt": np.broadcast_to(rt, (N, 128, N)).copy(), "rm": rm.astype(ml_dtypes.bfloat16), "w": rng.standard_normal((N, 128, 128), dtype=np.float32).astype(ml_dtypes.bfloat16)}
def setup_inputs_big(rng):
    d = setup_inputs(rng)
    for k in ("x", "w"): d[k] = (d[k].astype(np.float32) * 1024.0).astype(d[k].dtype)
    return d
def setup_inputs_small(rng):
    d = setup_inputs(rng)
    for k in ("x", "w"): d[k] = (d[k].astype(np.float32) * (1 / 1024.0)).astype(d[k].dtype)
    return d
def setup_inputs_apart(rng):
    d = setup_inputs(rng)
    f = (10.0 ** rng.permutation(np.linspace(-1.5, 1.5, N))).astype(np.float32).reshape(N, 1, 1)
    for k in ("x",): d[k] = (d[k].astype(np.float32) * f).astype(d[k].dtype)
    return d
def setup_inputs_faint(rng):
    d = setup_inputs(rng); x = d["x"].astype(np.float32); rt = d["rt"][0].astype(np.float32); t = int(rng.integers(N))
    p = rt @ np.linalg.solve(rt.T @ rt, np.ones(N, np.float32))
    x[t] = x[t] / 16 - np.outer(p, rng.uniform(20, 22, TOK).astype(np.float32))
    d["x"] = x.astype(d["x"].dtype)
    return d
def reference(x, rt, rm, w):
    X, RT, W = x.astype(np.float64), rt.astype(np.float64), w.astype(np.float64)
    y = np.zeros((N, 128, TOK))
    for r in range(N):
        sc = RT[r].T @ X[r]
        for t in range(TOK):
            ex = ROUTE[r][t]; g = sigmoid(sc[ex, t]); g = g / (g.sum() + EPS)
            y[r][:, t] = sum(g[i] * (W[e].T @ X[r][:, t]) for i, e in enumerate(ex))
    return {"y": y.astype(ml_dtypes.bfloat16)}

@@ -1,0 +1,206 @@
+from concourse.bass import DstId, RemoteDMATransfer
+from concourse.mybir import AluOpType, ActivationFunctionType
+
+NSIM = 512
+NR = 9
+D = 128
+NT = 256
+EPS = 0.01
+
+SCRATCH = {
+    "wall": ("sbuf", [128, NR * D], "bfloat16"),
+    "xs": ("sbuf", [128, NT], "bfloat16"),
+    "rts": ("sbuf", [128, 16], "bfloat16"),
+    "rms": ("sbuf", [128, NT], "bfloat16"),
+    "amx": ("sbuf", [128, NT], "bfloat16"),
+    "one": ("sbuf", [128, D], "bfloat16"),
+    "eye": ("sbuf", [128, 16], "bfloat16"),
+    "sel": ("sbuf", [128, NR * D], "bfloat16"),
+    "xg": ("sbuf", [128, NR * NT], "bfloat16"),
+    "rinv": ("sbuf", [128, NT], "float32"),
+    "ys": ("sbuf", [128, NT], "bfloat16"),
+    "ps_s": ("psum", [128, 512], "float32"),
+    "ps_d": ("psum", [128, 512], "float32"),
+    "ps_y": ("psum", [128, 512], "float32"),
+    "ps_b0": ("psum", [128, 512], "float32"),
+    "ps_b1": ("psum", [128, 512], "float32"),
+    "ps_b2": ("psum", [128, 512], "float32"),
+    "ps_b3": ("psum", [128, 512], "float32"),
+    "ps_b4": ("psum", [128, 512], "float32"),
+}
+SEMAPHORES = (["w_ld", "x_ld", "rm_ld", "c_one", "c_eps", "eye_ok", "sel_ok", "sc_ok", "sig_ok", "am_ok", "d_ok",
+               "r_ok", "y_ok", "ys_ok", "out_ok", "ls"]
+              + ["a%d" % e for e in range(NR)] + ["xg%d" % e for e in range(NR)] + ["bk%d" % k for k in range(5)])
+
+_CACHE = {}
+
+
+def _mask(topo, src, dests):
+    m = topo.mask(src, dests[0])
+    for d in dests[1:]:
+        m &= topo.mask(src, d)
+    return m
+
+
+def _plan(T, topo):
+    if "plan" in _CACHE:
+        return _CACHE["plan"]
+    cores = list(T.cores)
+    n = len(cores)
+    world = range(NSIM)
+    rank_hosts = sorted(set(topo.host(c) for c in cores))
+    spare = [h for h in sorted(set(topo.host(c) for c in world)) if h not in rank_hosts]
+    by_host = {h: [r for r in range(n) if topo.host(cores[r]) == h] for h in rank_hosts}
+    sends = {}
+    arr = {c: [] for c in cores}
+
+    def lanes(h, ch, die_first):
+        cs = [c for c in world if topo.host(c) == h and topo.chip(c) == ch]
+        mate = [m for m in world if topo.mates(cs[0], m)][0]
+        groups = {}
+        for c in cs:
+            groups.setdefault((topo.die(c) != die_first, topo.may_write(c, mate)), []).append(c)
+        return [groups[k] for k in sorted(groups)]
+
+    for r, s in enumerate(cores):
+        h = topo.host(s)
+        mine = by_host[h]
+        i = mine.index(r)
+        sem = "a%d" % r
+
+        def rot(lst):
+            return [lst[(i + j) % len(lst)] for j in range(len(lst))]
+
+        dests = []
+        far = [d for d in range(n) if not topo.may_write(s, cores[d])]
+        if far:
+            hh = [x for x in spare
+                  if all(topo.may_write(s, q) and topo.may_write(q, cores[far[0]])
+                         for q in world if topo.host(q) == x and topo.chip(q) == topo.chip(s))][0]
+            if topo.rack(hh) != topo.rack(h):
+                a = lanes(hh, topo.chip(s), topo.die(s))[0][1]
+                dests.append(a)
+                tg = rot(far)
+                sends.setdefault(a, []).append(dict(waits=[sem], lo=r, hi=r + 1, dests=[cores[d] for d in tg], sem=sem))
+                for j, d in enumerate(tg):
+                    arr[cores[d]].append((9 + j, sem, [r]))
+            else:
+                for j, d in enumerate(rot(far)):
+                    b = lanes(hh, topo.chip(cores[d]), topo.die(s))[i][0]
+                    dests.append(b)
+                    sends.setdefault(b, []).append(dict(waits=[sem], lo=r, hi=r + 1, dests=[cores[d]], sem=sem))
+                    arr[cores[d]].append((9 + j, sem, [r]))
+        near = rot(mine)[1:]
+        for h2 in rank_hosts:
+            if h2 != h and all(topo.same_plane(s, cores[d]) for d in by_host[h2]):
+                near += rot(by_host[h2])
+        for d in near:
+            dests.append(cores[d])
+            arr[cores[d]].append((len(dests), sem, [r]))
+        sends.setdefault(s, []).append(dict(waits=["w_ld"], lo=r, hi=r + 1, dests=dests, sem=sem))
+        for h2 in rank_hosts:
+            if topo.rack(h2) != topo.rack(h) and topo.may_write(s, cores[by_host[h2][0]]):
+                d = [q for q in by_host[h2] if topo.chip(cores[q]) == topo.chip(s)][0]
+                bsem = "a%d" % mine[0]
+                sends[s].append(dict(waits=["a%d" % p for p in mine if p != r], lo=mine[0], hi=mine[-1] + 1,
+                                     dests=[cores[d]], sem=bsem))
+                arr[cores[d]].append((7.5, bsem, list(mine)))
+
+    inc = {}
+    for c in sends:
+        for sd in sends[c]:
+            ne = bin(_mask(topo, c, sd["dests"])).count("1")
+            for d in sd["dests"]:
+                inc[(d, sd["sem"])] = inc.get((d, sd["sem"]), 0) + ne
+    for c in cores:
+        inc[(c, "w_ld")] = 16
+    order = {}
+    for r, c in enumerate(cores):
+        order[c] = [("w_ld", [r])] + [(sm, sl) for (_, sm, sl) in sorted(arr[c])]
+    _CACHE["plan"] = dict(sends=sends, inc=inc, order=order)
+    return _CACHE["plan"]
+
+
+def rank_program(g, core, T, topo):
+    plan = _plan(T, topo)
+    sends = plan["sends"].get(core, [])
+    inc = plan["inc"]
+    rank = T.rank_of(core)
+    if rank is None and not sends:
+        return
+    S = T.sem
+    n, n1 = NR, NR + 1
+    mult = AluOpType.mult
+
+    if rank is not None:
+        v, t, sc, sy = g.vector, g.tensor, g.scalar, g.sync
+        order = plan["order"][core]
+        seq = [e for (_, sl) in order for e in sl]
+        sy.dma_start(T.wall[:, rank * D:(rank + 1) * D], T.w[:, :]).then_inc(S.w_ld, 16)
+        sc.dma_start(T.xs[:, :], T.x[:, :]).then_inc(S.x_ld, 16)
+        sc.dma_start(T.rts[:, 0:n], T.rt[:, :]).then_inc(S.x_ld, 16)
+        sy.dma_start(T.rms[0:n, :], T.rm[:, :]).then_inc(S.rm_ld, 16)
+        v.memset(T.one[0:n1, :], 1.0).then_inc(S.c_one, 1)
+        v.memset(T.amx[0:n1, :], EPS).then_inc(S.c_eps, 1)
+        g.wait_ge(S.c_one, 1)
+        g.affine_select(T.eye[0:n1, 0:n1], T.one[0:n1, 0:n1], [[-1, n1]], AluOpType.is_equal, 0.0, 0, 1).then_inc(S.eye_ok, 1)
+        v.wait_ge(S.c_one, 1)
+        v.wait_ge(S.eye_ok, 1)
+        for e in range(n):
+            v.tensor_scalar(T.sel[0:n1, e * D:(e + 1) * D], T.one[0:n1, 0:D], T.eye[0:n1, e:e + 1], None, mult).then_inc(S.sel_ok, 1)
+        t.wait_ge(S.x_ld, 32)
+        t.matmul(T.ps_s[0:n, 0:NT], T.rts[:, 0:n], T.xs[:, :], True, True).then_inc(S.sc_ok, 1)
+        sc.wait_ge(S.sc_ok, 1)
+        sc.activation(T.ps_s[0:n, 0:NT], T.ps_s[0:n, 0:NT], ActivationFunctionType.Sigmoid).then_inc(S.sig_ok, 1)
+        v.wait_ge(S.sig_ok, 1)
+        v.wait_ge(S.rm_ld, 16)
+        v.wait_ge(S.c_eps, 1)
+        v.tensor_tensor(T.amx[0:n, :], T.ps_s[0:n, 0:NT], T.rms[0:n, :], mult).then_inc(S.am_ok, 1)
+        t.wait_ge(S.am_ok, 1)
+        t.wait_ge(S.sel_ok, n)
+        t.wait_ge(S.c_one, 1)
+        t.wait_ge(S.c_eps, 1)
+        for k, e in enumerate(seq):
+            o = (k % 2) * NT
+            t.matmul(T["ps_b%d" % (k // 2)][:, o:o + NT], T.sel[0:n1, e * D:(e + 1) * D], T.amx[0:n1, :], True, True).then_inc(S["bk%d" % (k // 2)], 1)
+        t.matmul(T.ps_d[:, 0:NT], T.one[0:n1, 0:D], T.amx[0:n1, :], True, True).then_inc(S.d_ok, 1)
+        v.wait_ge(S.x_ld, 32)
+        for k, e in enumerate(seq):
+            o = (k % 2) * NT
+            if k % 2 == 0:
+                v.wait_ge(S["bk%d" % (k // 2)], min(2, n - k))
+            v.tensor_tensor(T.xg[:, e * NT:(e + 1) * NT], T["ps_b%d" % (k // 2)][:, o:o + NT], T.xs[:, :], mult).then_inc(S["xg%d" % e], 1)
+        v.wait_ge(S.d_ok, 1)
+        v.reciprocal(T.rinv[:, :], T.ps_d[:, 0:NT]).then_inc(S.r_ok, 1)
+        k = 0
+        last = None
+        for (sm, sl) in order:
+            t.wait_ge(S[sm], inc[(core, sm)])
+            for e in sl:
+                t.wait_ge(S["xg%d" % e], 1)
+                last = t.matmul(T.ps_y[:, 0:NT], T.wall[:, e * D:(e + 1) * D], T.xg[:, e * NT:(e + 1) * NT], k == 0, k == n - 1)
+                k += 1
+        last.then_inc(S.y_ok, 1)
+        v.wait_ge(S.y_ok, 1)
+        v.wait_ge(S.r_ok, 1)
+        v.tensor_tensor(T.ys[:, :], T.ps_y[:, 0:NT], T.rinv[:, :], mult).then_inc(S.ys_ok, 1)
+        sy.wait_ge(S.ys_ok, 1)
+        sy.dma_start(T.y[:, :], T.ys[:, :]).then_inc(S.out_ok, 16)
+        sy.wait_ge(S.out_ok, 16)
+
+    left = 0
+    for sd in sends:
+        for sm in sd["waits"]:
+            g.wait_ge(S[sm], inc[(core, sm)])
+        ap = T.wall[:, sd["lo"] * D:sd["hi"] * D]
+        m = _mask(topo, core, sd["dests"])
+        ids = [topo.addr(d, core) for d in sd["dests"]]
+        if len(ids) == 1:
+            g.remote_dma(out_ap=ap, in_ap=ap, remote_sem=S[sd["sem"]], local_sem=S.ls, pid=ids[0][1],
+                         routing_id=ids[0][0], dma_engine_mask=m)
+        else:
+            g.remote_dma_fused([RemoteDMATransfer(dst_ids=[DstId(rid=a, pnc=p) for (a, p) in ids], dma_engine_mask=m,
+                                                  remote_sem=S[sd["sem"]], srcs=[ap], dsts=[ap for _ in ids], alu_op=0)],
+                               local_sem=S.ls)
+        left += bin(m).count("1")
+    g.wait_ge(S.ls, left)

@@ -5,6 +5,7 @@ NSIM = 512
 NR = 9
 D = 128
 NT = 256
+NB = NT // D
 EPS = 0.01
 
 SCRATCH = {
@@ -14,7 +15,9 @@ SCRATCH = {
     "rms": ("sbuf", [128, NT], "bfloat16"),
     "amx": ("sbuf", [128, NT], "bfloat16"),
     "one": ("sbuf", [128, D], "bfloat16"),
-    "eye": ("sbuf", [128, 16], "bfloat16"),
+    "eye": ("sbuf", [128, D], "bfloat16"),
+    "rcol": ("sbuf", [128, 4], "float32"),
+    "rb": ("sbuf", [128, NT], "bfloat16"),
     "sel": ("sbuf", [128, NR * D], "bfloat16"),
     "xg": ("sbuf", [128, NR * NT], "bfloat16"),
     "rinv": ("sbuf", [128, NT], "float32"),
@@ -29,7 +32,7 @@ SCRATCH = {
     "ps_b4": ("psum", [128, 512], "float32"),
 }
 SEMAPHORES = (["w_ld", "x_ld", "rm_ld", "c_one", "c_eps", "eye_ok", "sel_ok", "sc_ok", "sig_ok", "am_ok", "d_ok",
-               "r_ok", "y_ok", "ys_ok", "out_ok", "ls"]
+               "r_ok", "rb_ok", "rr_ok", "rc_ok", "y_ok", "ys_ok", "out_ok", "ls"]
               + ["a%d" % e for e in range(NR)] + ["xg%d" % e for e in range(NR)] + ["bk%d" % k for k in range(5)])
 
 _CACHE = {}
@@ -52,6 +55,7 @@ def _plan(T, topo):
     spare = [h for h in sorted(set(topo.host(c) for c in world)) if h not in rank_hosts]
     by_host = {h: [r for r in range(n) if topo.host(cores[r]) == h] for h in rank_hosts}
     sends = {}
+    late = []
     arr = {c: [] for c in cores}
 
     def lanes(h, ch, die_first):
@@ -77,19 +81,27 @@ def _plan(T, topo):
             hh = [x for x in spare
                   if all(topo.may_write(s, q) and topo.may_write(q, cores[far[0]])
                          for q in world if topo.host(q) == x and topo.chip(q) == topo.chip(s))][0]
-            if topo.rack(hh) != topo.rack(h):
-                a = lanes(hh, topo.chip(s), topo.die(s))[0][1]
-                dests.append(a)
-                tg = rot(far)
-                sends.setdefault(a, []).append(dict(waits=[sem], lo=r, hi=r + 1, dests=[cores[d] for d in tg], sem=sem))
-                for j, d in enumerate(tg):
-                    arr[cores[d]].append((9 + j, sem, [r]))
-            else:
-                for j, d in enumerate(rot(far)):
-                    b = lanes(hh, topo.chip(cores[d]), topo.die(s))[i][0]
-                    dests.append(b)
-                    sends.setdefault(b, []).append(dict(waits=[sem], lo=r, hi=r + 1, dests=[cores[d]], sem=sem))
-                    arr[cores[d]].append((9 + j, sem, [r]))
+            tg = rot(far)
+            cable_first = topo.rack(hh) != topo.rack(h)
+            for j, part in enumerate((tg[0::2], tg[1::2])):
+                if cable_first:
+                    q = lanes(hh, topo.chip(s), topo.die(s))[j][1]
+                else:
+                    q = lanes(hh, topo.chip(cores[part[0]]), topo.die(s))[j][0]
+                dests.append(q)
+                sends.setdefault(q, []).append(dict(waits=[sem], lo=r, hi=r + 1, dests=[cores[d] for d in part], sem=sem))
+                for jj, d in enumerate(part):
+                    arr[cores[d]].append((9 + j + jj, sem, [r]))
+        for h2 in rank_hosts:
+            if topo.rack(h2) != topo.rack(h) and topo.may_write(s, cores[by_host[h2][0]]):
+                hp = by_host[h2]
+                d = [q for q in hp if topo.chip(cores[q]) == topo.chip(s)][0]
+                dests.append(cores[d])
+                arr[cores[d]].append((len(dests), sem, [r]))
+                others = [hp[(hp.index(d) + j) % len(hp)] for j in range(1, len(hp))]
+                late.append((cores[d], dict(waits=[sem], lo=r, hi=r + 1, dests=[cores[p] for p in others], sem=sem)))
+                for p in others:
+                    arr[cores[p]].append((8.5, sem, [r]))
         near = rot(mine)[1:]
         for h2 in rank_hosts:
             if h2 != h and all(topo.same_plane(s, cores[d]) for d in by_host[h2]):
@@ -98,13 +110,8 @@ def _plan(T, topo):
             dests.append(cores[d])
             arr[cores[d]].append((len(dests), sem, [r]))
         sends.setdefault(s, []).append(dict(waits=["w_ld"], lo=r, hi=r + 1, dests=dests, sem=sem))
-        for h2 in rank_hosts:
-            if topo.rack(h2) != topo.rack(h) and topo.may_write(s, cores[by_host[h2][0]]):
-                d = [q for q in by_host[h2] if topo.chip(cores[q]) == topo.chip(s)][0]
-                bsem = "a%d" % mine[0]
-                sends[s].append(dict(waits=["a%d" % p for p in mine if p != r], lo=mine[0], hi=mine[-1] + 1,
-                                     dests=[cores[d]], sem=bsem))
-                arr[cores[d]].append((7.5, bsem, list(mine)))
+    for (c, sd) in late:
+        sends[c].append(sd)
 
     inc = {}
     for c in sends:
@@ -140,10 +147,10 @@ def rank_program(g, core, T, topo):
         sc.dma_start(T.xs[:, :], T.x[:, :]).then_inc(S.x_ld, 16)
         sc.dma_start(T.rts[:, 0:n], T.rt[:, :]).then_inc(S.x_ld, 16)
         sy.dma_start(T.rms[0:n, :], T.rm[:, :]).then_inc(S.rm_ld, 16)
-        v.memset(T.one[0:n1, :], 1.0).then_inc(S.c_one, 1)
+        v.memset(T.one[:, :], 1.0).then_inc(S.c_one, 1)
         v.memset(T.amx[0:n1, :], EPS).then_inc(S.c_eps, 1)
         g.wait_ge(S.c_one, 1)
-        g.affine_select(T.eye[0:n1, 0:n1], T.one[0:n1, 0:n1], [[-1, n1]], AluOpType.is_equal, 0.0, 0, 1).then_inc(S.eye_ok, 1)
+        g.affine_select(T.eye[:, :], T.one[:, :], [[-1, D]], AluOpType.is_equal, 0.0, 0, 1).then_inc(S.eye_ok, 1)
         v.wait_ge(S.c_one, 1)
         v.wait_ge(S.eye_ok, 1)
         for e in range(n):
@@ -160,18 +167,28 @@ def rank_program(g, core, T, topo):
         t.wait_ge(S.sel_ok, n)
         t.wait_ge(S.c_one, 1)
         t.wait_ge(S.c_eps, 1)
+        t.wait_ge(S.eye_ok, 1)
+        for b in range(NB):
+            t.matmul(T.ps_d[:, b:b + 1], T.amx[0:n1, b * D:(b + 1) * D], T.one[0:n1, 0:1], True, True).then_inc(S.d_ok, 1)
+        v.wait_ge(S.d_ok, NB)
+        v.reciprocal(T.rcol[:, 0:NB], T.ps_d[:, 0:NB]).then_inc(S.r_ok, 1)
+        v.wait_ge(S.r_ok, 1)
+        for b in range(NB):
+            v.tensor_scalar(T.rb[:, b * D:(b + 1) * D], T.one[:, :], T.rcol[:, b:b + 1], None, mult).then_inc(S.rb_ok, 1)
         for k, e in enumerate(seq):
             o = (k % 2) * NT
             t.matmul(T["ps_b%d" % (k // 2)][:, o:o + NT], T.sel[0:n1, e * D:(e + 1) * D], T.amx[0:n1, :], True, True).then_inc(S["bk%d" % (k // 2)], 1)
-        t.matmul(T.ps_d[:, 0:NT], T.one[0:n1, 0:D], T.amx[0:n1, :], True, True).then_inc(S.d_ok, 1)
+        t.wait_ge(S.rb_ok, NB)
+        for b in range(NB):
+            t.matmul(T.ps_d[:, NT + b * D:NT + (b + 1) * D], T.rb[:, b * D:(b + 1) * D], T.eye[:, :], True, True).then_inc(S.rr_ok, 1)
+        sc.wait_ge(S.rr_ok, NB)
+        sc.activation(T.rinv[:, :], T.ps_d[:, NT:2 * NT], ActivationFunctionType.Copy).then_inc(S.rc_ok, 1)
         v.wait_ge(S.x_ld, 32)
         for k, e in enumerate(seq):
             o = (k % 2) * NT
             if k % 2 == 0:
                 v.wait_ge(S["bk%d" % (k // 2)], min(2, n - k))
             v.tensor_tensor(T.xg[:, e * NT:(e + 1) * NT], T["ps_b%d" % (k // 2)][:, o:o + NT], T.xs[:, :], mult).then_inc(S["xg%d" % e], 1)
-        v.wait_ge(S.d_ok, 1)
-        v.reciprocal(T.rinv[:, :], T.ps_d[:, 0:NT]).then_inc(S.r_ok, 1)
         k = 0
         last = None
         for (sm, sl) in order:
@@ -182,7 +199,7 @@ def rank_program(g, core, T, topo):
                 k += 1
         last.then_inc(S.y_ok, 1)
         v.wait_ge(S.y_ok, 1)
-        v.wait_ge(S.r_ok, 1)
+        v.wait_ge(S.rc_ok, 1)
         v.tensor_tensor(T.ys[:, :], T.ps_y[:, 0:NT], T.rinv[:, :], mult).then_inc(S.ys_ok, 1)
         sy.wait_ge(S.ys_ok, 1)
         sy.dma_start(T.y[:, :], T.ys[:, :]).then_inc(S.out_ok, 16)

@@ -32,7 +32,7 @@ SCRATCH = {
     "ps_b4": ("psum", [128, 512], "float32"),
 }
 SEMAPHORES = (["w_ld", "x_ld", "rm_ld", "c_one", "c_eps", "eye_ok", "sel_ok", "sc_ok", "sig_ok", "am_ok", "d_ok",
-               "r_ok", "rb_ok", "rr_ok", "rc_ok", "y_ok", "ys_ok", "out_ok", "ls"]
+               "r_ok", "rb_ok", "rr_ok", "rc_ok", "y_ok0", "y_ok1", "ys_ok0", "ys_ok1", "out_ok0", "out_ok1", "ls"]
               + ["a%d" % e for e in range(NR)] + ["xg%d" % e for e in range(NR)] + ["bk%d" % k for k in range(5)])
 
 _CACHE = {}
@@ -83,17 +83,19 @@ def _plan(T, topo):
                          for q in world if topo.host(q) == x and topo.chip(q) == topo.chip(s))][0]
             tg = rot(far)
             cable_first = topo.rack(hh) != topo.rack(h)
-            for j, part in enumerate((tg[0::2], tg[1::2])):
+            for j, part in enumerate((tg,) if cable_first else tuple([d] for d in tg)):
                 if cable_first:
                     q = lanes(hh, topo.chip(s), topo.die(s))[j][1]
                 else:
-                    q = lanes(hh, topo.chip(cores[part[0]]), topo.die(s))[j][0]
+                    q = lanes(hh, topo.chip(cores[part[0]]), topo.die(s))[i][0]
                 dests.append(q)
                 sends.setdefault(q, []).append(dict(waits=[sem], lo=r, hi=r + 1, dests=[cores[d] for d in part], sem=sem))
                 for jj, d in enumerate(part):
                     arr[cores[d]].append((9 + j + jj, sem, [r]))
+        duty = False
         for h2 in rank_hosts:
             if topo.rack(h2) != topo.rack(h) and topo.may_write(s, cores[by_host[h2][0]]):
+                duty = True
                 hp = by_host[h2]
                 d = [q for q in hp if topo.chip(cores[q]) == topo.chip(s)][0]
                 dests.append(cores[d])
@@ -105,7 +107,13 @@ def _plan(T, topo):
         near = rot(mine)[1:]
         for h2 in rank_hosts:
             if h2 != h and all(topo.same_plane(s, cores[d]) for d in by_host[h2]):
-                near += rot(by_host[h2])
+                oth = rot(by_host[h2])
+                if duty and not any(topo.rack(h3) != topo.rack(h2) and topo.may_write(cores[oth[0]], cores[by_host[h3][0]])
+                                    for h3 in rank_hosts):
+                    late.append((cores[oth[0]], dict(waits=[sem], lo=r, hi=r + 1, dests=[cores[oth[-1]]], sem=sem)))
+                    arr[cores[oth[-1]]].append((8.5, sem, [r]))
+                    oth = oth[:-1]
+                near += oth
         for d in near:
             dests.append(cores[d])
             arr[cores[d]].append((len(dests), sem, [r]))
@@ -189,21 +197,24 @@ def rank_program(g, core, T, topo):
             if k % 2 == 0:
                 v.wait_ge(S["bk%d" % (k // 2)], min(2, n - k))
             v.tensor_tensor(T.xg[:, e * NT:(e + 1) * NT], T["ps_b%d" % (k // 2)][:, o:o + NT], T.xs[:, :], mult).then_inc(S["xg%d" % e], 1)
+        acc = [T.ps_y[:, 0:D], T.ps_s[:, NT:NT + D]]
         k = 0
-        last = None
+        last = [None, None]
         for (sm, sl) in order:
             t.wait_ge(S[sm], inc[(core, sm)])
             for e in sl:
                 t.wait_ge(S["xg%d" % e], 1)
-                last = t.matmul(T.ps_y[:, 0:NT], T.wall[:, e * D:(e + 1) * D], T.xg[:, e * NT:(e + 1) * NT], k == 0, k == n - 1)
+                for b in range(NB):
+                    last[b] = t.matmul(acc[b], T.wall[:, e * D:(e + 1) * D], T.xg[:, e * NT + b * D:e * NT + (b + 1) * D], k == 0, k == n - 1)
                 k += 1
-        last.then_inc(S.y_ok, 1)
-        v.wait_ge(S.y_ok, 1)
         v.wait_ge(S.rc_ok, 1)
-        v.tensor_tensor(T.ys[:, :], T.ps_y[:, 0:NT], T.rinv[:, :], mult).then_inc(S.ys_ok, 1)
-        sy.wait_ge(S.ys_ok, 1)
-        sy.dma_start(T.y[:, :], T.ys[:, :]).then_inc(S.out_ok, 16)
-        sy.wait_ge(S.out_ok, 16)
+        for b, q in enumerate((sy, sc)):
+            last[b].then_inc(S["y_ok%d" % b], 1)
+            v.wait_ge(S["y_ok%d" % b], 1)
+            v.tensor_tensor(T.ys[:, b * D:(b + 1) * D], acc[b], T.rinv[:, b * D:(b + 1) * D], mult).then_inc(S["ys_ok%d" % b], 1)
+            q.wait_ge(S["ys_ok%d" % b], 1)
+            q.dma_start(T.y[:, b * D:(b + 1) * D], T.ys[:, b * D:(b + 1) * D]).then_inc(S["out_ok%d" % b], 16)
+            q.wait_ge(S["out_ok%d" % b], 16)
 
     left = 0
     for sd in sends:

from concourse.bass import DstId, RemoteDMATransfer
from concourse.mybir import AluOpType, ActivationFunctionType

NSIM = 512
NR = 9
D = 128
NT = 256
NB = NT // D
EPS = 0.01

SCRATCH = {
    "wall": ("sbuf", [128, NR * D], "bfloat16"),
    "xs": ("sbuf", [128, NT], "bfloat16"),
    "rts": ("sbuf", [128, 16], "bfloat16"),
    "rms": ("sbuf", [128, NT], "bfloat16"),
    "amx": ("sbuf", [128, NT], "bfloat16"),
    "one": ("sbuf", [128, D], "bfloat16"),
    "eye": ("sbuf", [128, D], "bfloat16"),
    "rcol": ("sbuf", [128, 4], "float32"),
    "rb": ("sbuf", [128, NT], "bfloat16"),
    "sel": ("sbuf", [128, NR * D], "bfloat16"),
    "xg": ("sbuf", [128, NR * NT], "bfloat16"),
    "rinv": ("sbuf", [128, NT], "float32"),
    "ys": ("sbuf", [128, NT], "bfloat16"),
    "ps_s": ("psum", [128, 512], "float32"),
    "ps_d": ("psum", [128, 512], "float32"),
    "ps_y": ("psum", [128, 512], "float32"),
    "ps_b0": ("psum", [128, 512], "float32"),
    "ps_b1": ("psum", [128, 512], "float32"),
    "ps_b2": ("psum", [128, 512], "float32"),
    "ps_b3": ("psum", [128, 512], "float32"),
    "ps_b4": ("psum", [128, 512], "float32"),
}
SEMAPHORES = (["w_ld", "x_ld", "rm_ld", "c_one", "c_eps", "eye_ok", "sel_ok", "sc_ok", "sig_ok", "am_ok", "d_ok",
               "r_ok", "rb_ok", "rr_ok", "rc_ok", "y_ok0", "y_ok1", "ys_ok0", "ys_ok1", "out_ok0", "out_ok1", "ls"]
              + ["a%d" % e for e in range(NR)] + ["xg%d" % e for e in range(NR)] + ["bk%d" % k for k in range(5)])

_CACHE = {}


def _mask(topo, src, dests):
    m = topo.mask(src, dests[0])
    for d in dests[1:]:
        m &= topo.mask(src, d)
    return m


def _plan(T, topo):
    if "plan" in _CACHE:
        return _CACHE["plan"]
    cores = list(T.cores)
    n = len(cores)
    world = range(NSIM)
    rank_hosts = sorted(set(topo.host(c) for c in cores))
    spare = [h for h in sorted(set(topo.host(c) for c in world)) if h not in rank_hosts]
    by_host = {h: [r for r in range(n) if topo.host(cores[r]) == h] for h in rank_hosts}
    sends = {}
    late = []
    arr = {c: [] for c in cores}

    def lanes(h, ch, die_first):
        cs = [c for c in world if topo.host(c) == h and topo.chip(c) == ch]
        mate = [m for m in world if topo.mates(cs[0], m)][0]
        groups = {}
        for c in cs:
            groups.setdefault((topo.die(c) != die_first, topo.may_write(c, mate)), []).append(c)
        return [groups[k] for k in sorted(groups)]

    for r, s in enumerate(cores):
        h = topo.host(s)
        mine = by_host[h]
        i = mine.index(r)
        sem = "a%d" % r

        def rot(lst):
            return [lst[(i + j) % len(lst)] for j in range(len(lst))]

        dests = []
        far = [d for d in range(n) if not topo.may_write(s, cores[d])]
        if far:
            hh = [x for x in spare
                  if all(topo.may_write(s, q) and topo.may_write(q, cores[far[0]])
                         for q in world if topo.host(q) == x and topo.chip(q) == topo.chip(s))][0]
            tg = rot(far)
            cable_first = topo.rack(hh) != topo.rack(h)
            for j, part in enumerate((tg,) if cable_first else tuple([d] for d in tg)):
                if cable_first:
                    q = lanes(hh, topo.chip(s), topo.die(s))[j][1]
                else:
                    q = lanes(hh, topo.chip(cores[part[0]]), topo.die(s))[i][0]
                dests.append(q)
                sends.setdefault(q, []).append(dict(waits=[sem], lo=r, hi=r + 1, dests=[cores[d] for d in part], sem=sem))
                for jj, d in enumerate(part):
                    arr[cores[d]].append((9 + j + jj, sem, [r]))
        duty = False
        for h2 in rank_hosts:
            if topo.rack(h2) != topo.rack(h) and topo.may_write(s, cores[by_host[h2][0]]):
                duty = True
                hp = by_host[h2]
                d = [q for q in hp if topo.chip(cores[q]) == topo.chip(s)][0]
                dests.append(cores[d])
                arr[cores[d]].append((len(dests), sem, [r]))
                others = [hp[(hp.index(d) + j) % len(hp)] for j in range(1, len(hp))]
                late.append((cores[d], dict(waits=[sem], lo=r, hi=r + 1, dests=[cores[p] for p in others], sem=sem)))
                for p in others:
                    arr[cores[p]].append((8.5, sem, [r]))
        near = rot(mine)[1:]
        for h2 in rank_hosts:
            if h2 != h and all(topo.same_plane(s, cores[d]) for d in by_host[h2]):
                oth = rot(by_host[h2])
                if duty and not any(topo.rack(h3) != topo.rack(h2) and topo.may_write(cores[oth[0]], cores[by_host[h3][0]])
                                    for h3 in rank_hosts):
                    late.append((cores[oth[0]], dict(waits=[sem], lo=r, hi=r + 1, dests=[cores[oth[-1]]], sem=sem)))
                    arr[cores[oth[-1]]].append((8.5, sem, [r]))
                    oth = oth[:-1]
                near += oth
        for d in near:
            dests.append(cores[d])
            arr[cores[d]].append((len(dests), sem, [r]))
        sends.setdefault(s, []).append(dict(waits=["w_ld"], lo=r, hi=r + 1, dests=dests, sem=sem))
    for (c, sd) in late:
        sends[c].append(sd)

    inc = {}
    for c in sends:
        for sd in sends[c]:
            ne = bin(_mask(topo, c, sd["dests"])).count("1")
            for d in sd["dests"]:
                inc[(d, sd["sem"])] = inc.get((d, sd["sem"]), 0) + ne
    for c in cores:
        inc[(c, "w_ld")] = 16
    order = {}
    for r, c in enumerate(cores):
        order[c] = [("w_ld", [r])] + [(sm, sl) for (_, sm, sl) in sorted(arr[c])]
    _CACHE["plan"] = dict(sends=sends, inc=inc, order=order)
    return _CACHE["plan"]


def rank_program(g, core, T, topo):
    plan = _plan(T, topo)
    sends = plan["sends"].get(core, [])
    inc = plan["inc"]
    rank = T.rank_of(core)
    if rank is None and not sends:
        return
    S = T.sem
    n, n1 = NR, NR + 1
    mult = AluOpType.mult

    if rank is not None:
        v, t, sc, sy = g.vector, g.tensor, g.scalar, g.sync
        order = plan["order"][core]
        seq = [e for (_, sl) in order for e in sl]
        sy.dma_start(T.wall[:, rank * D:(rank + 1) * D], T.w[:, :]).then_inc(S.w_ld, 16)
        sc.dma_start(T.xs[:, :], T.x[:, :]).then_inc(S.x_ld, 16)
        sc.dma_start(T.rts[:, 0:n], T.rt[:, :]).then_inc(S.x_ld, 16)
        sy.dma_start(T.rms[0:n, :], T.rm[:, :]).then_inc(S.rm_ld, 16)
        v.memset(T.one[:, :], 1.0).then_inc(S.c_one, 1)
        v.memset(T.amx[0:n1, :], EPS).then_inc(S.c_eps, 1)
        g.wait_ge(S.c_one, 1)
        g.affine_select(T.eye[:, :], T.one[:, :], [[-1, D]], AluOpType.is_equal, 0.0, 0, 1).then_inc(S.eye_ok, 1)
        v.wait_ge(S.c_one, 1)
        v.wait_ge(S.eye_ok, 1)
        for e in range(n):
            v.tensor_scalar(T.sel[0:n1, e * D:(e + 1) * D], T.one[0:n1, 0:D], T.eye[0:n1, e:e + 1], None, mult).then_inc(S.sel_ok, 1)
        t.wait_ge(S.x_ld, 32)
        t.matmul(T.ps_s[0:n, 0:NT], T.rts[:, 0:n], T.xs[:, :], True, True).then_inc(S.sc_ok, 1)
        sc.wait_ge(S.sc_ok, 1)
        sc.activation(T.ps_s[0:n, 0:NT], T.ps_s[0:n, 0:NT], ActivationFunctionType.Sigmoid).then_inc(S.sig_ok, 1)
        v.wait_ge(S.sig_ok, 1)
        v.wait_ge(S.rm_ld, 16)
        v.wait_ge(S.c_eps, 1)
        v.tensor_tensor(T.amx[0:n, :], T.ps_s[0:n, 0:NT], T.rms[0:n, :], mult).then_inc(S.am_ok, 1)
        t.wait_ge(S.am_ok, 1)
        t.wait_ge(S.sel_ok, n)
        t.wait_ge(S.c_one, 1)
        t.wait_ge(S.c_eps, 1)
        t.wait_ge(S.eye_ok, 1)
        for b in range(NB):
            t.matmul(T.ps_d[:, b:b + 1], T.amx[0:n1, b * D:(b + 1) * D], T.one[0:n1, 0:1], True, True).then_inc(S.d_ok, 1)
        v.wait_ge(S.d_ok, NB)
        v.reciprocal(T.rcol[:, 0:NB], T.ps_d[:, 0:NB]).then_inc(S.r_ok, 1)
        v.wait_ge(S.r_ok, 1)
        for b in range(NB):
            v.tensor_scalar(T.rb[:, b * D:(b + 1) * D], T.one[:, :], T.rcol[:, b:b + 1], None, mult).then_inc(S.rb_ok, 1)
        for k, e in enumerate(seq):
            o = (k % 2) * NT
            t.matmul(T["ps_b%d" % (k // 2)][:, o:o + NT], T.sel[0:n1, e * D:(e + 1) * D], T.amx[0:n1, :], True, True).then_inc(S["bk%d" % (k // 2)], 1)
        t.wait_ge(S.rb_ok, NB)
        for b in range(NB):
            t.matmul(T.ps_d[:, NT + b * D:NT + (b + 1) * D], T.rb[:, b * D:(b + 1) * D], T.eye[:, :], True, True).then_inc(S.rr_ok, 1)
        sc.wait_ge(S.rr_ok, NB)
        sc.activation(T.rinv[:, :], T.ps_d[:, NT:2 * NT], ActivationFunctionType.Copy).then_inc(S.rc_ok, 1)
        v.wait_ge(S.x_ld, 32)
        for k, e in enumerate(seq):
            o = (k % 2) * NT
            if k % 2 == 0:
                v.wait_ge(S["bk%d" % (k // 2)], min(2, n - k))
            v.tensor_tensor(T.xg[:, e * NT:(e + 1) * NT], T["ps_b%d" % (k // 2)][:, o:o + NT], T.xs[:, :], mult).then_inc(S["xg%d" % e], 1)
        acc = [T.ps_y[:, 0:D], T.ps_s[:, NT:NT + D]]
        k = 0
        last = [None, None]
        for (sm, sl) in order:
            t.wait_ge(S[sm], inc[(core, sm)])
            for e in sl:
                t.wait_ge(S["xg%d" % e], 1)
                for b in range(NB):
                    last[b] = t.matmul(acc[b], T.wall[:, e * D:(e + 1) * D], T.xg[:, e * NT + b * D:e * NT + (b + 1) * D], k == 0, k == n - 1)
                k += 1
        v.wait_ge(S.rc_ok, 1)
        for b, q in enumerate((sy, sc)):
            last[b].then_inc(S["y_ok%d" % b], 1)
            v.wait_ge(S["y_ok%d" % b], 1)
            v.tensor_tensor(T.ys[:, b * D:(b + 1) * D], acc[b], T.rinv[:, b * D:(b + 1) * D], mult).then_inc(S["ys_ok%d" % b], 1)
            q.wait_ge(S["ys_ok%d" % b], 1)
            q.dma_start(T.y[:, b * D:(b + 1) * D], T.ys[:, b * D:(b + 1) * D]).then_inc(S["out_ok%d" % b], 16)
            q.wait_ge(S["out_ok%d" % b], 16)

    left = 0
    for sd in sends:
        for sm in sd["waits"]:
            g.wait_ge(S[sm], inc[(core, sm)])
        ap = T.wall[:, sd["lo"] * D:sd["hi"] * D]
        m = _mask(topo, core, sd["dests"])
        ids = [topo.addr(d, core) for d in sd["dests"]]
        if len(ids) == 1:
            g.remote_dma(out_ap=ap, in_ap=ap, remote_sem=S[sd["sem"]], local_sem=S.ls, pid=ids[0][1],
                         routing_id=ids[0][0], dma_engine_mask=m)
        else:
            g.remote_dma_fused([RemoteDMATransfer(dst_ids=[DstId(rid=a, pnc=p) for (a, p) in ids], dma_engine_mask=m,
                                                  remote_sem=S[sd["sem"]], srcs=[ap], dsts=[ap for _ in ids], alu_op=0)],
                               local_sem=S.ls)
        left += bin(m).count("1")
    g.wait_ge(S.ls, left)
